import numpy as np
import ml_dtypes


def mxq(x, axis, fmt="e4m3"):
    dtype, down = {"e4m3": (ml_dtypes.float8_e4m3fn, 7), "e5m2": (ml_dtypes.float8_e5m2, 14)}[fmt]
    v = np.moveaxis(np.asarray(x, np.float32).astype(ml_dtypes.bfloat16).astype(np.float64), axis, -1)
    blocks = v.reshape(v.shape[:-1] + (-1, 32))
    amax = np.abs(blocks).max(-1, keepdims=True)
    byte = np.maximum(np.where(amax > 0, np.frexp(amax)[1] - 1 + 127, 0) - down, 1)
    scale = np.exp2(byte - 127.0)
    codes = (blocks / scale).astype(np.float32).astype(dtype).astype(np.float64)
    return np.moveaxis((codes * scale).reshape(v.shape), -1, axis)


WIDE = False


def mx_kscale(k):
    if not WIDE:
        return np.ones(k)
    levels = np.array([10, -10, 5, -5, 0])
    if k % 512:
        return np.exp2(np.random.permutation(np.resize(levels, k // 32))).repeat(32)
    a = np.empty((k // 512, 16))
    for p in range(k // 512):
        a[p, :8] = np.random.permutation(np.resize(levels, 8))
        for g in range(8):
            far = levels[np.abs(levels - a[p, g]) >= 10]
            a[p, g + 8] = far[np.random.randint(len(far))]
    return np.exp2(a.ravel()).repeat(32)


def f64(x):
    return np.asarray(x).astype(np.float64)


def striped(idx):
    return np.tile(idx.reshape(-1, 16).T, (8, 1)).astype(np.uint16)


def unstriped(offs):
    return offs[:16].T.reshape(-1).astype(np.int64)


def gelu(v):
    return 0.5 * v * (1.0 + np.tanh(np.sqrt(2.0 / np.pi) * (v + 0.044715 * v**3)))


K, T, E, C, N = 2048, 512, 4, 256, 256


def by_expert(wq, xq):
    return np.concatenate([wq[e].T @ xq[:, e * C:(e + 1) * C] for e in range(E)], axis=1)


def setup_inputs():
    n = np.random.standard_normal
    s = mx_kscale(K)[:, None]
    first = np.random.permutation(np.repeat(np.arange(E), T // E))
    second = (first + 1 + np.random.permutation(np.repeat(np.arange(E - 1), -(-T // (E - 1)))[:T])) % E
    while np.bincount(second, minlength=E).max() != T // E:
        load = np.bincount(second, minlength=E); hi, lo = int(load.argmax()), int(load.argmin())
        t = np.flatnonzero((second == hi) & (first != lo))[0]; second[t] = lo
    slot_token = np.empty(E * C, np.int64); pos = np.empty((2, T), np.int64); fill = np.zeros(E, np.int64)
    place = np.stack([np.random.permutation(C) for _ in range(E)])
    for r, deal in enumerate((first, second)):
        for t in np.random.permutation(T):
            e = deal[t]; j = e * C + place[e, fill[e]]; fill[e] += 1; slot_token[j] = t; pos[r, t] = j
    g = np.random.uniform(0.2, 0.8, T)
    return {
        "xT": (n((K, T)) * s).astype(np.float32),
        "w": (n((E, K, N)) / np.sqrt(K) / s[None]).astype(np.float32),
        "b": (0.3 * n((N, E))).astype(np.float32),
        "gate": np.stack([np.tile(g, (N, 1)), np.tile(1.0 - g, (N, 1))]).astype(np.float32),
        "offs": striped(slot_token),
        "pos1": striped(pos[0]),
        "pos2": striped(pos[1]),
    }


def reference(xT, w, b, gate, offs, pos1, pos2):
    idx = unstriped(offs)
    xq = mxq(f64(xT)[:, idx], 0, "e4m3")
    y = by_expert(mxq(f64(w), 1, "e4m3"), xq)
    y = gelu(y + np.repeat(f64(b), C, axis=1))
    return f64(gate[0]) * y[:, unstriped(pos1)] + f64(gate[1]) * y[:, unstriped(pos2)]

@@ -1,0 +1,149 @@
+from contextlib import ExitStack
+
+import concourse.mybir as mybir
+
+K, T, E, C, N = 2048, 512, 4, 256, 256
+FLOPS = 2 * E * C * K * N
+
+F32 = mybir.dt.float32
+BF16 = mybir.dt.bfloat16
+U32 = mybir.dt.uint32
+U16 = mybir.dt.uint16
+U8 = mybir.dt.uint8
+FP8X4 = mybir.dt.float8_e4m3fn_x4
+MULT = mybir.AluOpType.mult
+ADD = mybir.AluOpType.add
+GELU = mybir.ActivationFunctionType.Gelu_apprx_tanh
+
+P = 128
+PACK = 4
+K_PASS = P * PACK
+PASSES = K // K_PASS
+BLOCKS = N // P
+SLOTS = E * C
+GATHERS = ((0, 384), (384, 768), (768, 1024))
+
+
+def tile_routed_moe_kernel(tc, xT, w, b, gate, offs, pos1, pos2, out):
+    nc = tc.nc
+
+    def interleave(engine, grouped, raw):
+        dst = grouped.rearrange("p (c i) t -> p c t i", i=4)
+        src = raw.rearrange("p t (c i) -> p c t i", i=4)
+        if engine == "vector":
+            nc.vector.tensor_copy(out=dst, in_=src)
+        else:
+            nc.scalar.copy(out=dst, in_=src)
+
+    with ExitStack() as ctx:
+        keep = ctx.enter_context(tc.tile_pool(name="keep", bufs=1))
+        psum = ctx.enter_context(tc.psum_pool(name="psum", bufs=1))
+
+        offs_sb = keep.tile([P, SLOTS // 16], U16, name="offs_sb")
+        pos1_sb = keep.tile([P, T // 16], U16, name="pos1_sb")
+        pos2_sb = keep.tile([P, T // 16], U16, name="pos2_sb")
+        bias = keep.tile([P, BLOCKS, E], F32, name="bias")
+        warm = keep.tile([P, 1], F32, name="warm")
+        warmed = keep.tile([P, 1], F32, name="warmed")
+
+        x_raw = [keep.tile([P, PACK, T], F32, name=f"x_raw{a}") for a in range(PASSES)]
+        x_grp = [keep.tile([P, T, PACK], BF16, name=f"x_grp{a}", align_bytes=64) for a in range(PASSES)]
+        x_words = [keep.tile([P, T], U32, name=f"x_words{a}", align_bytes=64) for a in range(PASSES)]
+        x_bytes = keep.tile([P, T], U8, name="x_bytes", align_bytes=64)
+        words = keep.tile([P, PASSES, SLOTS], U32, name="words", align_bytes=64)
+        scales = keep.tile([P, SLOTS], U8, name="scales", align_bytes=64)
+        y = [keep.tile([P, SLOTS], F32, name=f"y{m}") for m in range(BLOCKS)]
+        gates = [keep.tile([P, 2, T], F32, name=f"gates{m}") for m in range(BLOCKS)]
+
+        for a in range(PASSES):
+            rows = xT[a * K_PASS : (a + 1) * K_PASS, :]
+            nc.sync.dma_start(out=x_raw[a][:], in_=rows.rearrange("(p j) t -> p j t", j=PACK))
+            if a == 0:
+                nc.sync.dma_start(offs_sb[:], offs)
+        nc.gpsimd.dma_start(out=bias[:], in_=b.rearrange("(m p) e -> p m e", p=P))
+        nc.gpsimd.memset(warm[:], 0.0)
+        nc.gpsimd.memset(x_bytes[:], 0)
+        nc.scalar.activation(out=warmed[:], in_=warm[:], func=GELU)
+
+        w_raw = {}
+        for e in range(E):
+            for h in range(2):
+                raw = keep.tile([P, 2, PACK, N], F32, name=f"w_raw{e}{h}")
+                w_raw[e, h] = raw
+                rows = w[e, 2 * h * K_PASS : (2 * h + 2) * K_PASS, :]
+                if (e, h) == (E - 1, 1):
+                    for a in range(2):
+                        nc.sync.dma_start(
+                            out=raw[:, a],
+                            in_=rows[a * K_PASS : (a + 1) * K_PASS, :].rearrange("(p j) n -> p j n", j=PACK),
+                        )
+                else:
+                    nc.sync.dma_start(out=raw[:], in_=rows.rearrange("(a p j) n -> p a j n", p=P, j=PACK))
+            if e == 0:
+                nc.sync.dma_start(pos1_sb[:], pos1)
+                nc.sync.dma_start(pos2_sb[:], pos2)
+        for m in range(BLOCKS):
+            nc.sync.dma_start(out=gates[m][:], in_=gate[:, m * P : (m + 1) * P, :].rearrange("g p t -> p g t"))
+
+        for a in range(PASSES):
+            interleave("vector", x_grp[a][:, 0:256, :], x_raw[a][:, :, 0:256])
+            interleave("scalar", x_grp[a][:, 256:512, :], x_raw[a][:, :, 256:512])
+            nc.vector.quantize_mx(
+                out=x_words[a][:].bitcast(FP8X4),
+                scales=x_bytes[4 * a :, :],
+                in_=x_grp[a][:].rearrange("p t j -> p (t j)"),
+            )
+            for lo, hi in GATHERS:
+                nc.vector.tensor_copy(words[:, a, lo:hi], x_words[a][:].indirect(offs_sb[:, lo // 16 : hi // 16]))
+        for lo, hi in GATHERS:
+            nc.vector.tensor_copy(scales[:, lo:hi], x_bytes[:].indirect(offs_sb[:, lo // 16 : hi // 16]))
+
+        for e in range(E):
+            slots = slice(e * C, (e + 1) * C)
+            acc = [psum.tile([P, C], F32, name=f"acc{e}{m}") for m in range(BLOCKS)]
+            for h in range(2):
+                last = (e, h) == (E - 1, 1)
+                grp = keep.tile([P, 2, N, PACK], BF16, name=f"w_grp{e}{h}", align_bytes=64)
+                codes = keep.tile([P, 2, N], U32, name=f"w_codes{e}{h}", align_bytes=64)
+                planes = keep.tile([P, 2, N], U8, name=f"w_planes{e}{h}", align_bytes=64)
+                for a in range(2):
+                    if last:
+                        interleave("scalar", grp[:, a, 0:P, :], w_raw[e, h][:, a, :, 0:P])
+                        interleave("vector", grp[:, a, P:N, :], w_raw[e, h][:, a, :, P:N])
+                        nc.vector.quantize_mx(
+                            out=codes[:, a].bitcast(FP8X4),
+                            scales=planes[:, a],
+                            in_=grp[:, a].rearrange("p n j -> p (n j)"),
+                        )
+                    else:
+                        interleave("scalar", grp[:, a], w_raw[e, h][:, a])
+                if not last:
+                    nc.vector.quantize_mx(
+                        out=codes[:].rearrange("p a n -> p (a n)").bitcast(FP8X4),
+                        scales=planes[:].rearrange("p a n -> p (a n)"),
+                        in_=grp[:].rearrange("p a n j -> p (a n j)"),
+                    )
+                for a in range(2):
+                    k = 2 * h + a
+                    for m in range(BLOCKS):
+                        cols = slice(m * P, (m + 1) * P)
+                        nc.tensor.matmul_mx(
+                            out=acc[m][:],
+                            lhsT=codes[:, a, cols].bitcast(FP8X4),
+                            lhsT_scale=planes[:, a, cols],
+                            rhs=words[:, k, slots].bitcast(FP8X4),
+                            rhs_scale=scales[4 * k :, slots],
+                            start=(k == 0),
+                            stop=(k == PASSES - 1),
+                        )
+            for m in range(BLOCKS):
+                nc.scalar.activation(out=y[m][:, slots], in_=acc[m][:], func=GELU, bias=bias[:, m, e : e + 1])
+
+        for m in range(BLOCKS):
+            first = keep.tile([P, T], F32, name=f"first{m}")
+            second = keep.tile([P, T], F32, name=f"second{m}")
+            total = keep.tile([P, T], F32, name=f"total{m}")
+            nc.vector.tensor_tensor(first[:], y[m][:].indirect(pos1_sb[:]), gates[m][:, 0], MULT)
+            nc.vector.tensor_tensor(second[:], y[m][:].indirect(pos2_sb[:]), gates[m][:, 1], MULT)
+            nc.vector.tensor_tensor(total[:], first[:], second[:], ADD)
+            nc.sync.dma_start(out=out[m * P : (m + 1) * P, :], in_=total[:])

@@ -21,17 +21,23 @@ K_PASS = P * PACK
 PASSES = K // K_PASS
 BLOCKS = N // P
 SLOTS = E * C
-GATHERS = ((0, 384), (384, 768), (768, 1024))
+WINDOW = 1376
 
 
 def tile_routed_moe_kernel(tc, xT, w, b, gate, offs, pos1, pos2, out):
     nc = tc.nc
 
     def interleave(engine, grouped, raw):
-        dst = grouped.rearrange("p (c i) t -> p c t i", i=4)
-        src = raw.rearrange("p t (c i) -> p c t i", i=4)
-        if engine == "vector":
+        if len(raw.shape) == 4:
+            dst = grouped.rearrange("p a (c i) t -> p a c t i", i=4)
+            src = raw.rearrange("p a t (c i) -> p a c t i", i=4)
+        else:
+            dst = grouped.rearrange("p (c i) t -> p c t i", i=4)
+            src = raw.rearrange("p t (c i) -> p c t i", i=4)
+        if engine == "V":
             nc.vector.tensor_copy(out=dst, in_=src)
+        elif engine == "G":
+            nc.gpsimd.tensor_scalar(out=dst, in0=src, scalar1=1.0, scalar2=0.0, op0=MULT, op1=ADD)
         else:
             nc.scalar.copy(out=dst, in_=src)
 
@@ -46,99 +52,159 @@ def tile_routed_moe_kernel(tc, xT, w, b, gate, offs, pos1, pos2, out):
         warm = keep.tile([P, 1], F32, name="warm")
         warmed = keep.tile([P, 1], F32, name="warmed")
 
-        x_raw = [keep.tile([P, PACK, T], F32, name=f"x_raw{a}") for a in range(PASSES)]
-        x_grp = [keep.tile([P, T, PACK], BF16, name=f"x_grp{a}", align_bytes=64) for a in range(PASSES)]
-        x_words = [keep.tile([P, T], U32, name=f"x_words{a}", align_bytes=64) for a in range(PASSES)]
-        x_bytes = keep.tile([P, T], U8, name="x_bytes", align_bytes=64)
+        x_words = [keep.tile([P, WINDOW], U32, name=f"x_words{a}", align_bytes=64) for a in range(PASSES)]
+        x_bytes = keep.tile([P, WINDOW], U8, name="x_bytes", align_bytes=64)
         words = keep.tile([P, PASSES, SLOTS], U32, name="words", align_bytes=64)
         scales = keep.tile([P, SLOTS], U8, name="scales", align_bytes=64)
         y = [keep.tile([P, SLOTS], F32, name=f"y{m}") for m in range(BLOCKS)]
         gates = [keep.tile([P, 2, T], F32, name=f"gates{m}") for m in range(BLOCKS)]
 
-        for a in range(PASSES):
-            rows = xT[a * K_PASS : (a + 1) * K_PASS, :]
-            nc.sync.dma_start(out=x_raw[a][:], in_=rows.rearrange("(p j) t -> p j t", j=PACK))
-            if a == 0:
-                nc.sync.dma_start(offs_sb[:], offs)
-        nc.gpsimd.dma_start(out=bias[:], in_=b.rearrange("(m p) e -> p m e", p=P))
-        nc.gpsimd.memset(warm[:], 0.0)
         nc.gpsimd.memset(x_bytes[:], 0)
+        nc.gpsimd.memset(warm[:], 0.0)
         nc.scalar.activation(out=warmed[:], in_=warm[:], func=GELU)
 
-        w_raw = {}
-        for e in range(E):
-            for h in range(2):
-                raw = keep.tile([P, 2, PACK, N], F32, name=f"w_raw{e}{h}")
-                w_raw[e, h] = raw
-                rows = w[e, 2 * h * K_PASS : (2 * h + 2) * K_PASS, :]
-                if (e, h) == (E - 1, 1):
-                    for a in range(2):
-                        nc.sync.dma_start(
-                            out=raw[:, a],
-                            in_=rows[a * K_PASS : (a + 1) * K_PASS, :].rearrange("(p j) n -> p j n", j=PACK),
-                        )
-                else:
-                    nc.sync.dma_start(out=raw[:], in_=rows.rearrange("(a p j) n -> p a j n", p=P, j=PACK))
-            if e == 0:
-                nc.sync.dma_start(pos1_sb[:], pos1)
-                nc.sync.dma_start(pos2_sb[:], pos2)
+        def x_load(raw, a, cols):
+            rows = xT[a * K_PASS : (a + 1) * K_PASS, :].rearrange("(p j) t -> p j t", j=PACK)
+            nc.sync.dma_start(out=raw[:], in_=rows[:, :, cols])
+
+        def w_load(raw, e, k, passes):
+            rows = w[e, k * K_PASS : (k + passes) * K_PASS, :]
+            nc.sync.dma_start(out=raw[:], in_=rows.rearrange("(a p j) n -> p a j n", p=P, j=PACK))
+
+        def quantise(codes, planes, grouped):
+            nc.vector.quantize_mx(out=codes.bitcast(FP8X4), scales=planes, in_=grouped)
+
+        x_raw00 = keep.tile([P, PACK, 256], F32)
+        x_load(x_raw00, 0, slice(0, 256))
+        x_raw01 = keep.tile([P, PACK, 256], F32)
+        x_load(x_raw01, 0, slice(256, 512))
+        nc.sync.dma_start(offs_sb[:], offs)
+        x_raw10 = keep.tile([P, PACK, 512], F32)
+        x_load(x_raw10, 1, slice(0, 512))
+        x_raw20 = keep.tile([P, PACK, 512], F32)
+        x_load(x_raw20, 2, slice(0, 512))
+        x_raw30 = keep.tile([P, PACK, 512], F32)
+        x_load(x_raw30, 3, slice(0, 512))
+        w_raw00 = keep.tile([P, 2, PACK, N], F32)
+        w_load(w_raw00, 0, 0, 2)
+        w_raw02 = keep.tile([P, 2, PACK, N], F32)
+        w_load(w_raw02, 0, 2, 2)
+        nc.sync.dma_start(pos1_sb[:], pos1)
+        nc.sync.dma_start(pos2_sb[:], pos2)
+        nc.sync.dma_start(out=bias[:], in_=b.rearrange("(m p) e -> p m e", p=P))
+        w_raw10 = keep.tile([P, 2, PACK, N], F32)
+        w_load(w_raw10, 1, 0, 2)
+        w_raw12 = keep.tile([P, 2, PACK, N], F32)
+        w_load(w_raw12, 1, 2, 2)
+        w_raw20 = keep.tile([P, 2, PACK, N], F32)
+        w_load(w_raw20, 2, 0, 2)
+        w_raw22 = keep.tile([P, 2, PACK, N], F32)
+        w_load(w_raw22, 2, 2, 2)
+        w_raw30 = keep.tile([P, 2, PACK, N], F32)
+        w_load(w_raw30, 3, 0, 2)
+        w_raw32 = keep.tile([P, 1, PACK, N], F32)
+        w_load(w_raw32, 3, 2, 1)
+        w_raw33 = keep.tile([P, 1, PACK, N], F32)
+        w_load(w_raw33, 3, 3, 1)
         for m in range(BLOCKS):
             nc.sync.dma_start(out=gates[m][:], in_=gate[:, m * P : (m + 1) * P, :].rearrange("g p t -> p g t"))
+        x_grp00 = keep.tile([P, 256, PACK], BF16, align_bytes=64)
+        interleave("V", x_grp00[:], x_raw00[:])
+        quantise(x_words[0][:, 0:256], x_bytes[4 * 0 :, 0:256], x_grp00[:].rearrange("p t j -> p (t j)"))
+        x_grp01 = keep.tile([P, 256, PACK], BF16, align_bytes=64)
+        interleave("S", x_grp01[:], x_raw01[:])
+        quantise(x_words[0][:, 256:512], x_bytes[4 * 0 :, 256:512], x_grp01[:].rearrange("p t j -> p (t j)"))
+        nc.vector.tensor_copy(words[:, 0, :], x_words[0][:].indirect(offs_sb[:]))
+        x_grp10 = keep.tile([P, 512, PACK], BF16, align_bytes=64)
+        interleave("S", x_grp10[:], x_raw10[:])
+        quantise(x_words[1][:, 0:512], x_bytes[4 * 1 :, 0:512], x_grp10[:].rearrange("p t j -> p (t j)"))
+        nc.vector.tensor_copy(words[:, 1, :], x_words[1][:].indirect(offs_sb[:]))
+        x_grp20 = keep.tile([P, 512, PACK], BF16, align_bytes=64)
+        interleave("S", x_grp20[:], x_raw20[:])
+        quantise(x_words[2][:, 0:512], x_bytes[4 * 2 :, 0:512], x_grp20[:].rearrange("p t j -> p (t j)"))
+        nc.vector.tensor_copy(words[:, 2, :], x_words[2][:].indirect(offs_sb[:]))
+        x_grp30 = keep.tile([P, 512, PACK], BF16, align_bytes=64)
+        interleave("S", x_grp30[:], x_raw30[:])
+        quantise(x_words[3][:, 0:512], x_bytes[4 * 3 :, 0:512], x_grp30[:].rearrange("p t j -> p (t j)"))
+        nc.vector.tensor_copy(words[:, 3, :], x_words[3][:].indirect(offs_sb[:]))
+        nc.vector.tensor_copy(scales[:], x_bytes[:].indirect(offs_sb[:]))
+        acc = [[psum.tile([P, C], F32, name=f"acc{e}{m}") for m in range(BLOCKS)] for e in range(E)]
 
-        for a in range(PASSES):
-            interleave("vector", x_grp[a][:, 0:256, :], x_raw[a][:, :, 0:256])
-            interleave("scalar", x_grp[a][:, 256:512, :], x_raw[a][:, :, 256:512])
-            nc.vector.quantize_mx(
-                out=x_words[a][:].bitcast(FP8X4),
-                scales=x_bytes[4 * a :, :],
-                in_=x_grp[a][:].rearrange("p t j -> p (t j)"),
-            )
-            for lo, hi in GATHERS:
-                nc.vector.tensor_copy(words[:, a, lo:hi], x_words[a][:].indirect(offs_sb[:, lo // 16 : hi // 16]))
-        for lo, hi in GATHERS:
-            nc.vector.tensor_copy(scales[:, lo:hi], x_bytes[:].indirect(offs_sb[:, lo // 16 : hi // 16]))
-
-        for e in range(E):
+        def multiply(e, k, m, codes, planes):
             slots = slice(e * C, (e + 1) * C)
-            acc = [psum.tile([P, C], F32, name=f"acc{e}{m}") for m in range(BLOCKS)]
-            for h in range(2):
-                last = (e, h) == (E - 1, 1)
-                grp = keep.tile([P, 2, N, PACK], BF16, name=f"w_grp{e}{h}", align_bytes=64)
-                codes = keep.tile([P, 2, N], U32, name=f"w_codes{e}{h}", align_bytes=64)
-                planes = keep.tile([P, 2, N], U8, name=f"w_planes{e}{h}", align_bytes=64)
-                for a in range(2):
-                    if last:
-                        interleave("scalar", grp[:, a, 0:P, :], w_raw[e, h][:, a, :, 0:P])
-                        interleave("vector", grp[:, a, P:N, :], w_raw[e, h][:, a, :, P:N])
-                        nc.vector.quantize_mx(
-                            out=codes[:, a].bitcast(FP8X4),
-                            scales=planes[:, a],
-                            in_=grp[:, a].rearrange("p n j -> p (n j)"),
-                        )
-                    else:
-                        interleave("scalar", grp[:, a], w_raw[e, h][:, a])
-                if not last:
-                    nc.vector.quantize_mx(
-                        out=codes[:].rearrange("p a n -> p (a n)").bitcast(FP8X4),
-                        scales=planes[:].rearrange("p a n -> p (a n)"),
-                        in_=grp[:].rearrange("p a n j -> p (a n j)"),
-                    )
-                for a in range(2):
-                    k = 2 * h + a
-                    for m in range(BLOCKS):
-                        cols = slice(m * P, (m + 1) * P)
-                        nc.tensor.matmul_mx(
-                            out=acc[m][:],
-                            lhsT=codes[:, a, cols].bitcast(FP8X4),
-                            lhsT_scale=planes[:, a, cols],
-                            rhs=words[:, k, slots].bitcast(FP8X4),
-                            rhs_scale=scales[4 * k :, slots],
-                            start=(k == 0),
-                            stop=(k == PASSES - 1),
-                        )
-            for m in range(BLOCKS):
-                nc.scalar.activation(out=y[m][:, slots], in_=acc[m][:], func=GELU, bias=bias[:, m, e : e + 1])
+            nc.tensor.matmul_mx(
+                out=acc[e][m][:],
+                lhsT=codes.bitcast(FP8X4),
+                lhsT_scale=planes,
+                rhs=words[:, k, slots].bitcast(FP8X4),
+                rhs_scale=scales[4 * k :, slots],
+                start=(k == 0),
+                stop=(k == PASSES - 1),
+            )
 
+        w_grp0 = keep.tile([P, PASSES, N, PACK], BF16, align_bytes=64)
+        w_codes0 = keep.tile([P, PASSES, N], U32, align_bytes=64)
+        w_planes0 = keep.tile([P, PASSES, N], U8, align_bytes=64)
+        interleave("S", w_grp0[:, 0:2], w_raw00[:])
+        interleave("S", w_grp0[:, 2:4], w_raw02[:])
+        quantise(w_codes0[:].rearrange("p a n -> p (a n)"), w_planes0[:].rearrange("p a n -> p (a n)"), w_grp0[:].rearrange("p a n j -> p (a n j)"))
+        for k in range(PASSES):
+            for m in range(BLOCKS):
+                multiply(0, k, m, w_codes0[:, k, m * P : (m + 1) * P], w_planes0[:, k, m * P : (m + 1) * P])
+        for m in range(BLOCKS):
+            nc.scalar.activation(out=y[m][:, 0:256], in_=acc[0][m][:], func=GELU, bias=bias[:, m, 0:1])
+        w_grp1 = keep.tile([P, PASSES, N, PACK], BF16, align_bytes=64)
+        w_codes1 = keep.tile([P, PASSES, N], U32, align_bytes=64)
+        w_planes1 = keep.tile([P, PASSES, N], U8, align_bytes=64)
+        interleave("S", w_grp1[:, 0:2], w_raw10[:])
+        interleave("V", w_grp1[:, 2:4], w_raw12[:])
+        quantise(w_codes1[:].rearrange("p a n -> p (a n)"), w_planes1[:].rearrange("p a n -> p (a n)"), w_grp1[:].rearrange("p a n j -> p (a n j)"))
+        for k in range(PASSES):
+            for m in range(BLOCKS):
+                multiply(1, k, m, w_codes1[:, k, m * P : (m + 1) * P], w_planes1[:, k, m * P : (m + 1) * P])
+        for m in range(BLOCKS):
+            nc.scalar.activation(out=y[m][:, 256:512], in_=acc[1][m][:], func=GELU, bias=bias[:, m, 1:2])
+        w_grp2 = keep.tile([P, PASSES, N, PACK], BF16, align_bytes=64)
+        w_codes2 = keep.tile([P, PASSES, N], U32, align_bytes=64)
+        w_planes2 = keep.tile([P, PASSES, N], U8, align_bytes=64)
+        interleave("S", w_grp2[:, 0:2], w_raw20[:])
+        interleave("V", w_grp2[:, 2:4], w_raw22[:])
+        quantise(w_codes2[:].rearrange("p a n -> p (a n)"), w_planes2[:].rearrange("p a n -> p (a n)"), w_grp2[:].rearrange("p a n j -> p (a n j)"))
+        for k in range(PASSES):
+            for m in range(BLOCKS):
+                multiply(2, k, m, w_codes2[:, k, m * P : (m + 1) * P], w_planes2[:, k, m * P : (m + 1) * P])
+        for m in range(BLOCKS):
+            nc.scalar.activation(out=y[m][:, 512:768], in_=acc[2][m][:], func=GELU, bias=bias[:, m, 2:3])
+        w_grp30 = keep.tile([P, 2, N, PACK], BF16, align_bytes=64)
+        w_codes30 = keep.tile([P, 2, N], U32, align_bytes=64)
+        w_planes30 = keep.tile([P, 2, N], U8, align_bytes=64)
+        interleave("S", w_grp30[:], w_raw30[:])
+        quantise(w_codes30[:].rearrange("p a n -> p (a n)"), w_planes30[:].rearrange("p a n -> p (a n)"), w_grp30[:].rearrange("p a n j -> p (a n j)"))
+        for a in range(2):
+            for m in range(BLOCKS):
+                multiply(3, 0 + a, m, w_codes30[:, a, m * P : (m + 1) * P], w_planes30[:, a, m * P : (m + 1) * P])
+        w_grp32 = keep.tile([P, 1, N, PACK], BF16, align_bytes=64)
+        w_codes32 = keep.tile([P, 1, N], U32, align_bytes=64)
+        w_planes32 = keep.tile([P, 1, N], U8, align_bytes=64)
+        interleave("V", w_grp32[:], w_raw32[:])
+        quantise(w_codes32[:].rearrange("p a n -> p (a n)"), w_planes32[:].rearrange("p a n -> p (a n)"), w_grp32[:].rearrange("p a n j -> p (a n j)"))
+        for a in range(1):
+            for m in range(BLOCKS):
+                multiply(3, 2 + a, m, w_codes32[:, a, m * P : (m + 1) * P], w_planes32[:, a, m * P : (m + 1) * P])
+        w_grp330 = keep.tile([P, P, PACK], BF16, align_bytes=64)
+        w_codes330 = keep.tile([P, P], U32, align_bytes=64)
+        w_planes330 = keep.tile([P, P], U8, align_bytes=64)
+        interleave("S", w_grp330[:], w_raw33[:, 0, :, 0 * P : 1 * P])
+        quantise(w_codes330[:], w_planes330[:], w_grp330[:].rearrange("p n j -> p (n j)"))
+        multiply(3, 3, 0, w_codes330[:], w_planes330[:])
+        w_grp331 = keep.tile([P, P, PACK], BF16, align_bytes=64)
+        w_codes331 = keep.tile([P, P], U32, align_bytes=64)
+        w_planes331 = keep.tile([P, P], U8, align_bytes=64)
+        interleave("V", w_grp331[:], w_raw33[:, 0, :, 1 * P : 2 * P])
+        quantise(w_codes331[:], w_planes331[:], w_grp331[:].rearrange("p n j -> p (n j)"))
+        multiply(3, 3, 1, w_codes331[:], w_planes331[:])
+        for m in range(BLOCKS):
+            nc.scalar.activation(out=y[m][:, 768:1024], in_=acc[3][m][:], func=GELU, bias=bias[:, m, 3:4])
         for m in range(BLOCKS):
             first = keep.tile([P, T], F32, name=f"first{m}")
             second = keep.tile([P, T], F32, name=f"second{m}")

@@ -1,6 +1,7 @@
 from contextlib import ExitStack
 
 import concourse.mybir as mybir
+from concourse.masks import make_identity
 
 K, T, E, C, N = 2048, 512, 4, 256, 256
 FLOPS = 2 * E * C * K * N
@@ -37,7 +38,9 @@ def tile_routed_moe_kernel(tc, xT, w, b, gate, offs, pos1, pos2, out):
         if engine == "V":
             nc.vector.tensor_copy(out=dst, in_=src)
         elif engine == "G":
-            nc.gpsimd.tensor_scalar(out=dst, in0=src, scalar1=1.0, scalar2=0.0, op0=MULT, op1=ADD)
+            nc.gpsimd.tensor_scalar(
+                out=grouped[:, 0], in0=raw[:, 0].rearrange("p t n -> p n t"), scalar1=1.0, scalar2=0.0, op0=MULT, op1=ADD
+            )
         else:
             nc.scalar.copy(out=dst, in_=src)
 
@@ -63,6 +66,9 @@ def tile_routed_moe_kernel(tc, xT, w, b, gate, offs, pos1, pos2, out):
         nc.gpsimd.memset(warm[:], 0.0)
         nc.scalar.activation(out=warmed[:], in_=warm[:], func=GELU)
 
+        identity = keep.tile([P, P], F32, name="identity")
+        make_identity(nc, identity[:])
+
         def x_load(raw, a, cols):
             rows = xT[a * K_PASS : (a + 1) * K_PASS, :].rearrange("(p j) t -> p j t", j=PACK)
             nc.sync.dma_start(out=raw[:], in_=rows[:, :, cols])
@@ -87,27 +93,60 @@ def tile_routed_moe_kernel(tc, xT, w, b, gate, offs, pos1, pos2, out):
         x_load(x_raw30, 3, slice(0, 512))
         w_raw00 = keep.tile([P, 2, PACK, N], F32)
         w_load(w_raw00, 0, 0, 2)
-        w_raw02 = keep.tile([P, 2, PACK, N], F32)
-        w_load(w_raw02, 0, 2, 2)
+        w_raw01 = keep.tile([P, 2, PACK, N], F32)
+        w_load(w_raw01, 0, 2, 2)
         nc.sync.dma_start(pos1_sb[:], pos1)
         nc.sync.dma_start(pos2_sb[:], pos2)
         nc.sync.dma_start(out=bias[:], in_=b.rearrange("(m p) e -> p m e", p=P))
         w_raw10 = keep.tile([P, 2, PACK, N], F32)
         w_load(w_raw10, 1, 0, 2)
-        w_raw12 = keep.tile([P, 2, PACK, N], F32)
-        w_load(w_raw12, 1, 2, 2)
+        w_raw11 = keep.tile([P, 2, PACK, N], F32)
+        w_load(w_raw11, 1, 2, 2)
         w_raw20 = keep.tile([P, 2, PACK, N], F32)
         w_load(w_raw20, 2, 0, 2)
-        w_raw22 = keep.tile([P, 2, PACK, N], F32)
-        w_load(w_raw22, 2, 2, 2)
+        w_raw21 = keep.tile([P, 2, PACK, N], F32)
+        w_load(w_raw21, 2, 2, 2)
         w_raw30 = keep.tile([P, 2, PACK, N], F32)
         w_load(w_raw30, 3, 0, 2)
-        w_raw32 = keep.tile([P, 1, PACK, N], F32)
-        w_load(w_raw32, 3, 2, 1)
-        w_raw33 = keep.tile([P, 1, PACK, N], F32)
-        w_load(w_raw33, 3, 3, 1)
-        for m in range(BLOCKS):
-            nc.sync.dma_start(out=gates[m][:], in_=gate[:, m * P : (m + 1) * P, :].rearrange("g p t -> p g t"))
+        w_raw31 = keep.tile([P, 2, PACK, N], F32)
+        w_load(w_raw31, 3, 2, 2)
+        nc.sync.dma_start(out=gates[0][:], in_=gate[:, 0 * P : 1 * P, :].rearrange("g p t -> p g t"))
+        nc.sync.dma_start(out=gates[1][:], in_=gate[:, 1 * P : 2 * P, :].rearrange("g p t -> p g t"))
+        def multiply(acc, e, k, codes, planes):
+            slots = slice(e * C, (e + 1) * C)
+            nc.tensor.matmul_mx(
+                out=acc,
+                lhsT=codes.bitcast(FP8X4),
+                lhsT_scale=planes,
+                rhs=words[:, k, slots].bitcast(FP8X4),
+                rhs_scale=scales[4 * k :, slots],
+                start=(k == 0),
+                stop=(k == PASSES - 1),
+            )
+
+        def activate(e, m, acc):
+            nc.scalar.activation(out=y[m][:, e * C : (e + 1) * C], in_=acc, func=GELU, bias=bias[:, m, e : e + 1])
+
+        w_grp0 = keep.tile([P, PASSES, N, PACK], BF16, align_bytes=64)
+        w_codes0 = keep.tile([P, PASSES, N], U32, align_bytes=64)
+        w_planes0 = keep.tile([P, PASSES, N], U8, align_bytes=64)
+        acc0 = psum.tile([P, BLOCKS, C], F32)
+        w_grp1 = keep.tile([P, PASSES, N, PACK], BF16, align_bytes=64, tag="a")
+        w_codes1 = keep.tile([P, PASSES, N], U32, align_bytes=64)
+        w_planes1 = keep.tile([P, PASSES, N], U8, align_bytes=64)
+        acc1 = psum.tile([P, BLOCKS, C], F32)
+        w_grp2 = keep.tile([P, PASSES, N, PACK], BF16, align_bytes=64, tag="b")
+        w_codes2 = keep.tile([P, PASSES, N], U32, align_bytes=64)
+        w_planes2 = keep.tile([P, PASSES, N], U8, align_bytes=64)
+        acc2 = psum.tile([P, BLOCKS, C], F32)
+        w_codes30 = keep.tile([P, 2, N], U32, align_bytes=64)
+        w_planes30 = keep.tile([P, 2, N], U8, align_bytes=64)
+        w_grp32 = keep.tile([P, 1, N, PACK], BF16, align_bytes=64)
+        w_codes32 = keep.tile([P, 1, N], U32, align_bytes=64)
+        w_planes32 = keep.tile([P, 1, N], U8, align_bytes=64)
+        w_codes33 = keep.tile([P, 1, N], U32, align_bytes=64)
+        w_planes33 = keep.tile([P, 1, N], U8, align_bytes=64)
+        acc_last = [psum.tile([P, C], F32, name=f"acc_last{m}") for m in range(BLOCKS)]
         x_grp00 = keep.tile([P, 256, PACK], BF16, align_bytes=64)
         interleave("V", x_grp00[:], x_raw00[:])
         quantise(x_words[0][:, 0:256], x_bytes[4 * 0 :, 0:256], x_grp00[:].rearrange("p t j -> p (t j)"))
@@ -128,88 +167,63 @@ def tile_routed_moe_kernel(tc, xT, w, b, gate, offs, pos1, pos2, out):
         quantise(x_words[3][:, 0:512], x_bytes[4 * 3 :, 0:512], x_grp30[:].rearrange("p t j -> p (t j)"))
         nc.vector.tensor_copy(words[:, 3, :], x_words[3][:].indirect(offs_sb[:]))
         nc.vector.tensor_copy(scales[:], x_bytes[:].indirect(offs_sb[:]))
-        acc = [[psum.tile([P, C], F32, name=f"acc{e}{m}") for m in range(BLOCKS)] for e in range(E)]
-
-        def multiply(e, k, m, codes, planes):
-            slots = slice(e * C, (e + 1) * C)
-            nc.tensor.matmul_mx(
-                out=acc[e][m][:],
-                lhsT=codes.bitcast(FP8X4),
-                lhsT_scale=planes,
-                rhs=words[:, k, slots].bitcast(FP8X4),
-                rhs_scale=scales[4 * k :, slots],
-                start=(k == 0),
-                stop=(k == PASSES - 1),
-            )
-
-        w_grp0 = keep.tile([P, PASSES, N, PACK], BF16, align_bytes=64)
-        w_codes0 = keep.tile([P, PASSES, N], U32, align_bytes=64)
-        w_planes0 = keep.tile([P, PASSES, N], U8, align_bytes=64)
         interleave("S", w_grp0[:, 0:2], w_raw00[:])
-        interleave("S", w_grp0[:, 2:4], w_raw02[:])
+        interleave("S", w_grp0[:, 2:3], w_raw01[:, 0:1])
+        interleave("G", w_grp0[:, 3:4], w_raw01[:, 1:2])
         quantise(w_codes0[:].rearrange("p a n -> p (a n)"), w_planes0[:].rearrange("p a n -> p (a n)"), w_grp0[:].rearrange("p a n j -> p (a n j)"))
-        for k in range(PASSES):
-            for m in range(BLOCKS):
-                multiply(0, k, m, w_codes0[:, k, m * P : (m + 1) * P], w_planes0[:, k, m * P : (m + 1) * P])
         for m in range(BLOCKS):
-            nc.scalar.activation(out=y[m][:, 0:256], in_=acc[0][m][:], func=GELU, bias=bias[:, m, 0:1])
-        w_grp1 = keep.tile([P, PASSES, N, PACK], BF16, align_bytes=64)
-        w_codes1 = keep.tile([P, PASSES, N], U32, align_bytes=64)
-        w_planes1 = keep.tile([P, PASSES, N], U8, align_bytes=64)
+            for k in range(PASSES):
+                multiply(acc0[:, m], 0, k, w_codes0[:, k, m * P : (m + 1) * P], w_planes0[:, k, m * P : (m + 1) * P])
+        for m in range(BLOCKS):
+            activate(0, m, acc0[:, m])
         interleave("S", w_grp1[:, 0:2], w_raw10[:])
-        interleave("V", w_grp1[:, 2:4], w_raw12[:])
+        interleave("G", w_grp1[:, 2:3], w_raw11[:, 0:1])
+        interleave("G", w_grp1[:, 3:4], w_raw11[:, 1:2])
         quantise(w_codes1[:].rearrange("p a n -> p (a n)"), w_planes1[:].rearrange("p a n -> p (a n)"), w_grp1[:].rearrange("p a n j -> p (a n j)"))
-        for k in range(PASSES):
-            for m in range(BLOCKS):
-                multiply(1, k, m, w_codes1[:, k, m * P : (m + 1) * P], w_planes1[:, k, m * P : (m + 1) * P])
         for m in range(BLOCKS):
-            nc.scalar.activation(out=y[m][:, 256:512], in_=acc[1][m][:], func=GELU, bias=bias[:, m, 1:2])
-        w_grp2 = keep.tile([P, PASSES, N, PACK], BF16, align_bytes=64)
-        w_codes2 = keep.tile([P, PASSES, N], U32, align_bytes=64)
-        w_planes2 = keep.tile([P, PASSES, N], U8, align_bytes=64)
+            for k in range(PASSES):
+                multiply(acc1[:, m], 1, k, w_codes1[:, k, m * P : (m + 1) * P], w_planes1[:, k, m * P : (m + 1) * P])
+        for m in range(BLOCKS):
+            activate(1, m, acc1[:, m])
         interleave("S", w_grp2[:, 0:2], w_raw20[:])
-        interleave("V", w_grp2[:, 2:4], w_raw22[:])
+        interleave("S", w_grp2[:, 2:4], w_raw21[:])
+        w_grp30 = keep.tile([P, 2, N, PACK], BF16, align_bytes=64, tag="a")
+        interleave("V", w_grp30[:], w_raw30[:])
         quantise(w_codes2[:].rearrange("p a n -> p (a n)"), w_planes2[:].rearrange("p a n -> p (a n)"), w_grp2[:].rearrange("p a n j -> p (a n j)"))
-        for k in range(PASSES):
-            for m in range(BLOCKS):
-                multiply(2, k, m, w_codes2[:, k, m * P : (m + 1) * P], w_planes2[:, k, m * P : (m + 1) * P])
         for m in range(BLOCKS):
-            nc.scalar.activation(out=y[m][:, 512:768], in_=acc[2][m][:], func=GELU, bias=bias[:, m, 2:3])
-        w_grp30 = keep.tile([P, 2, N, PACK], BF16, align_bytes=64)
-        w_codes30 = keep.tile([P, 2, N], U32, align_bytes=64)
-        w_planes30 = keep.tile([P, 2, N], U8, align_bytes=64)
-        interleave("S", w_grp30[:], w_raw30[:])
+            for k in range(PASSES):
+                multiply(acc2[:, m], 2, k, w_codes2[:, k, m * P : (m + 1) * P], w_planes2[:, k, m * P : (m + 1) * P])
+        for m in range(BLOCKS):
+            activate(2, m, acc2[:, m])
         quantise(w_codes30[:].rearrange("p a n -> p (a n)"), w_planes30[:].rearrange("p a n -> p (a n)"), w_grp30[:].rearrange("p a n j -> p (a n j)"))
-        for a in range(2):
-            for m in range(BLOCKS):
-                multiply(3, 0 + a, m, w_codes30[:, a, m * P : (m + 1) * P], w_planes30[:, a, m * P : (m + 1) * P])
-        w_grp32 = keep.tile([P, 1, N, PACK], BF16, align_bytes=64)
-        w_codes32 = keep.tile([P, 1, N], U32, align_bytes=64)
-        w_planes32 = keep.tile([P, 1, N], U8, align_bytes=64)
-        interleave("V", w_grp32[:], w_raw32[:])
+        for m in range(BLOCKS):
+            for k in range(2):
+                multiply(acc_last[m][:], 3, k, w_codes30[:, k, m * P : (m + 1) * P], w_planes30[:, k, m * P : (m + 1) * P])
+        interleave("S", w_grp32[:], w_raw31[:, 0:1])
+        w_grp33 = keep.tile([P, 1, N, PACK], BF16, align_bytes=64, tag="b")
+        interleave("V", w_grp33[:], w_raw31[:, 1:2])
         quantise(w_codes32[:].rearrange("p a n -> p (a n)"), w_planes32[:].rearrange("p a n -> p (a n)"), w_grp32[:].rearrange("p a n j -> p (a n j)"))
-        for a in range(1):
-            for m in range(BLOCKS):
-                multiply(3, 2 + a, m, w_codes32[:, a, m * P : (m + 1) * P], w_planes32[:, a, m * P : (m + 1) * P])
-        w_grp330 = keep.tile([P, P, PACK], BF16, align_bytes=64)
-        w_codes330 = keep.tile([P, P], U32, align_bytes=64)
-        w_planes330 = keep.tile([P, P], U8, align_bytes=64)
-        interleave("S", w_grp330[:], w_raw33[:, 0, :, 0 * P : 1 * P])
-        quantise(w_codes330[:], w_planes330[:], w_grp330[:].rearrange("p n j -> p (n j)"))
-        multiply(3, 3, 0, w_codes330[:], w_planes330[:])
-        w_grp331 = keep.tile([P, P, PACK], BF16, align_bytes=64)
-        w_codes331 = keep.tile([P, P], U32, align_bytes=64)
-        w_planes331 = keep.tile([P, P], U8, align_bytes=64)
-        interleave("V", w_grp331[:], w_raw33[:, 0, :, 1 * P : 2 * P])
-        quantise(w_codes331[:], w_planes331[:], w_grp331[:].rearrange("p n j -> p (n j)"))
-        multiply(3, 3, 1, w_codes331[:], w_planes331[:])
         for m in range(BLOCKS):
-            nc.scalar.activation(out=y[m][:, 768:1024], in_=acc[3][m][:], func=GELU, bias=bias[:, m, 3:4])
+            multiply(acc_last[m][:], 3, 2, w_codes32[:, 0, m * P : (m + 1) * P], w_planes32[:, 0, m * P : (m + 1) * P])
+        quantise(w_codes33[:].rearrange("p a n -> p (a n)"), w_planes33[:].rearrange("p a n -> p (a n)"), w_grp33[:].rearrange("p a n j -> p (a n j)"))
         for m in range(BLOCKS):
-            first = keep.tile([P, T], F32, name=f"first{m}")
-            second = keep.tile([P, T], F32, name=f"second{m}")
-            total = keep.tile([P, T], F32, name=f"total{m}")
-            nc.vector.tensor_tensor(first[:], y[m][:].indirect(pos1_sb[:]), gates[m][:, 0], MULT)
-            nc.vector.tensor_tensor(second[:], y[m][:].indirect(pos2_sb[:]), gates[m][:, 1], MULT)
-            nc.vector.tensor_tensor(total[:], first[:], second[:], ADD)
-            nc.sync.dma_start(out=out[m * P : (m + 1) * P, :], in_=total[:])
+            multiply(acc_last[m][:], 3, 3, w_codes33[:, 0, m * P : (m + 1) * P], w_planes33[:, 0, m * P : (m + 1) * P])
+        activate(3, 0, acc_last[0][:])
+        activate(3, 1, acc_last[1][:])
+        first0 = keep.tile([P, T], F32)
+        second0 = keep.tile([P, T], F32)
+        total0 = keep.tile([P, T], F32)
+        nc.vector.tensor_tensor(first0[:], y[0][:].indirect(pos1_sb[:]), gates[0][:, 0], MULT)
+        nc.vector.tensor_tensor(second0[:], y[0][:].indirect(pos2_sb[:]), gates[0][:, 1], MULT)
+        both0 = psum.tile([P, T], F32)
+        nc.tensor.matmul(both0[:], identity[:], first0[:], start=True, stop=False)
+        nc.tensor.matmul(both0[:], identity[:], second0[:], start=False, stop=True)
+        nc.scalar.copy(out=total0[:], in_=both0[:])
+        nc.sync.dma_start(out=out[0 * P : 1 * P, :], in_=total0[:])
+        first1 = keep.tile([P, T], F32)
+        second1 = keep.tile([P, T], F32)
+        total1 = keep.tile([P, T], F32)
+        nc.vector.tensor_tensor(first1[:], y[1][:].indirect(pos1_sb[:]), gates[1][:, 0], MULT)
+        nc.vector.tensor_tensor(second1[:], y[1][:].indirect(pos2_sb[:]), gates[1][:, 1], MULT)
+        nc.vector.tensor_tensor(total1[:], first1[:], second1[:], ADD)
+        nc.sync.dma_start(out=out[1 * P : 2 * P, :], in_=total1[:])

@@ -95,9 +95,6 @@ def tile_routed_moe_kernel(tc, xT, w, b, gate, offs, pos1, pos2, out):
         w_load(w_raw00, 0, 0, 2)
         w_raw01 = keep.tile([P, 2, PACK, N], F32)
         w_load(w_raw01, 0, 2, 2)
-        nc.sync.dma_start(pos1_sb[:], pos1)
-        nc.sync.dma_start(pos2_sb[:], pos2)
-        nc.sync.dma_start(out=bias[:], in_=b.rearrange("(m p) e -> p m e", p=P))
         w_raw10 = keep.tile([P, 2, PACK, N], F32)
         w_load(w_raw10, 1, 0, 2)
         w_raw11 = keep.tile([P, 2, PACK, N], F32)
@@ -106,10 +103,13 @@ def tile_routed_moe_kernel(tc, xT, w, b, gate, offs, pos1, pos2, out):
         w_load(w_raw20, 2, 0, 2)
         w_raw21 = keep.tile([P, 2, PACK, N], F32)
         w_load(w_raw21, 2, 2, 2)
+        nc.sync.dma_start(out=bias[:], in_=b.rearrange("(m p) e -> p m e", p=P))
         w_raw30 = keep.tile([P, 2, PACK, N], F32)
         w_load(w_raw30, 3, 0, 2)
         w_raw31 = keep.tile([P, 2, PACK, N], F32)
         w_load(w_raw31, 3, 2, 2)
+        nc.sync.dma_start(pos1_sb[:], pos1)
+        nc.sync.dma_start(pos2_sb[:], pos2)
         nc.sync.dma_start(out=gates[0][:], in_=gate[:, 0 * P : 1 * P, :].rearrange("g p t -> p g t"))
         nc.sync.dma_start(out=gates[1][:], in_=gate[:, 1 * P : 2 * P, :].rearrange("g p t -> p g t"))
         def multiply(acc, e, k, codes, planes):
@@ -131,19 +131,21 @@ def tile_routed_moe_kernel(tc, xT, w, b, gate, offs, pos1, pos2, out):
         w_codes0 = keep.tile([P, PASSES, N], U32, align_bytes=64)
         w_planes0 = keep.tile([P, PASSES, N], U8, align_bytes=64)
         acc0 = psum.tile([P, BLOCKS, C], F32)
-        w_grp1 = keep.tile([P, PASSES, N, PACK], BF16, align_bytes=64, tag="a")
+        w_grp1 = keep.tile([P, PASSES, N, PACK], BF16, align_bytes=64)
         w_codes1 = keep.tile([P, PASSES, N], U32, align_bytes=64)
         w_planes1 = keep.tile([P, PASSES, N], U8, align_bytes=64)
         acc1 = psum.tile([P, BLOCKS, C], F32)
-        w_grp2 = keep.tile([P, PASSES, N, PACK], BF16, align_bytes=64, tag="b")
+        w_grp2 = keep.tile([P, PASSES, N, PACK], BF16, align_bytes=64)
         w_codes2 = keep.tile([P, PASSES, N], U32, align_bytes=64)
         w_planes2 = keep.tile([P, PASSES, N], U8, align_bytes=64)
         acc2 = psum.tile([P, BLOCKS, C], F32)
+        w_grp30 = keep.tile([P, 2, N, PACK], BF16, align_bytes=64)
         w_codes30 = keep.tile([P, 2, N], U32, align_bytes=64)
         w_planes30 = keep.tile([P, 2, N], U8, align_bytes=64)
         w_grp32 = keep.tile([P, 1, N, PACK], BF16, align_bytes=64)
         w_codes32 = keep.tile([P, 1, N], U32, align_bytes=64)
         w_planes32 = keep.tile([P, 1, N], U8, align_bytes=64)
+        w_grp33 = keep.tile([P, 1, N, PACK], BF16, align_bytes=64)
         w_codes33 = keep.tile([P, 1, N], U32, align_bytes=64)
         w_planes33 = keep.tile([P, 1, N], U8, align_bytes=64)
         acc_last = [psum.tile([P, C], F32, name=f"acc_last{m}") for m in range(BLOCKS)]
@@ -174,40 +176,38 @@ def tile_routed_moe_kernel(tc, xT, w, b, gate, offs, pos1, pos2, out):
         for m in range(BLOCKS):
             for k in range(PASSES):
                 multiply(acc0[:, m], 0, k, w_codes0[:, k, m * P : (m + 1) * P], w_planes0[:, k, m * P : (m + 1) * P])
-        for m in range(BLOCKS):
-            activate(0, m, acc0[:, m])
         interleave("S", w_grp1[:, 0:2], w_raw10[:])
-        interleave("G", w_grp1[:, 2:3], w_raw11[:, 0:1])
+        interleave("S", w_grp1[:, 2:3], w_raw11[:, 0:1])
         interleave("G", w_grp1[:, 3:4], w_raw11[:, 1:2])
         quantise(w_codes1[:].rearrange("p a n -> p (a n)"), w_planes1[:].rearrange("p a n -> p (a n)"), w_grp1[:].rearrange("p a n j -> p (a n j)"))
         for m in range(BLOCKS):
             for k in range(PASSES):
                 multiply(acc1[:, m], 1, k, w_codes1[:, k, m * P : (m + 1) * P], w_planes1[:, k, m * P : (m + 1) * P])
-        for m in range(BLOCKS):
-            activate(1, m, acc1[:, m])
         interleave("S", w_grp2[:, 0:2], w_raw20[:])
-        interleave("S", w_grp2[:, 2:4], w_raw21[:])
-        w_grp30 = keep.tile([P, 2, N, PACK], BF16, align_bytes=64, tag="a")
-        interleave("V", w_grp30[:], w_raw30[:])
+        interleave("V", w_grp2[:, 2:4], w_raw21[:])
         quantise(w_codes2[:].rearrange("p a n -> p (a n)"), w_planes2[:].rearrange("p a n -> p (a n)"), w_grp2[:].rearrange("p a n j -> p (a n j)"))
         for m in range(BLOCKS):
             for k in range(PASSES):
                 multiply(acc2[:, m], 2, k, w_codes2[:, k, m * P : (m + 1) * P], w_planes2[:, k, m * P : (m + 1) * P])
         for m in range(BLOCKS):
-            activate(2, m, acc2[:, m])
+            activate(0, m, acc0[:, m])
+        for m in range(BLOCKS):
+            activate(1, m, acc1[:, m])
+        interleave("S", w_grp30[:], w_raw30[:])
         quantise(w_codes30[:].rearrange("p a n -> p (a n)"), w_planes30[:].rearrange("p a n -> p (a n)"), w_grp30[:].rearrange("p a n j -> p (a n j)"))
         for m in range(BLOCKS):
             for k in range(2):
                 multiply(acc_last[m][:], 3, k, w_codes30[:, k, m * P : (m + 1) * P], w_planes30[:, k, m * P : (m + 1) * P])
-        interleave("S", w_grp32[:], w_raw31[:, 0:1])
-        w_grp33 = keep.tile([P, 1, N, PACK], BF16, align_bytes=64, tag="b")
-        interleave("V", w_grp33[:], w_raw31[:, 1:2])
+        interleave("V", w_grp32[:], w_raw31[:, 0:1])
+        interleave("S", w_grp33[:], w_raw31[:, 1:2])
         quantise(w_codes32[:].rearrange("p a n -> p (a n)"), w_planes32[:].rearrange("p a n -> p (a n)"), w_grp32[:].rearrange("p a n j -> p (a n j)"))
         for m in range(BLOCKS):
             multiply(acc_last[m][:], 3, 2, w_codes32[:, 0, m * P : (m + 1) * P], w_planes32[:, 0, m * P : (m + 1) * P])
         quantise(w_codes33[:].rearrange("p a n -> p (a n)"), w_planes33[:].rearrange("p a n -> p (a n)"), w_grp33[:].rearrange("p a n j -> p (a n j)"))
         for m in range(BLOCKS):
             multiply(acc_last[m][:], 3, 3, w_codes33[:, 0, m * P : (m + 1) * P], w_planes33[:, 0, m * P : (m + 1) * P])
+        for m in range(BLOCKS):
+            activate(2, m, acc2[:, m])
         activate(3, 0, acc_last[0][:])
         activate(3, 1, acc_last[1][:])
         first0 = keep.tile([P, T], F32)

@@ -1,7 +1,6 @@
 from contextlib import ExitStack
 
 import concourse.mybir as mybir
-from concourse.masks import make_identity
 
 K, T, E, C, N = 2048, 512, 4, 256, 256
 FLOPS = 2 * E * C * K * N
@@ -22,102 +21,107 @@ K_PASS = P * PACK
 PASSES = K // K_PASS
 BLOCKS = N // P
 SLOTS = E * C
+LAST = E - 1
+
 WINDOW = 1376
+
+TOKEN_ENGINES = ("vector", "scalar", "scalar", "scalar")
+WEIGHT_ENGINES = (
+    (("scalar", 0, 2), ("scalar", 2, 1), ("gpsimd", 3, 1)),
+    (("scalar", 0, 2), ("scalar", 2, 1), ("gpsimd", 3, 1)),
+    (("scalar", 0, 2), ("vector", 2, 2)),
+)
 
 
 def tile_routed_moe_kernel(tc, xT, w, b, gate, offs, pos1, pos2, out):
     nc = tc.nc
 
-    def interleave(engine, grouped, raw):
-        if len(raw.shape) == 4:
-            dst = grouped.rearrange("p a (c i) t -> p a c t i", i=4)
-            src = raw.rearrange("p a t (c i) -> p a c t i", i=4)
-        else:
-            dst = grouped.rearrange("p (c i) t -> p c t i", i=4)
-            src = raw.rearrange("p t (c i) -> p c t i", i=4)
-        if engine == "V":
-            nc.vector.tensor_copy(out=dst, in_=src)
-        elif engine == "G":
-            nc.gpsimd.tensor_scalar(
-                out=grouped[:, 0], in0=raw[:, 0].rearrange("p t n -> p n t"), scalar1=1.0, scalar2=0.0, op0=MULT, op1=ADD
-            )
-        else:
-            nc.scalar.copy(out=dst, in_=src)
-
     with ExitStack() as ctx:
         keep = ctx.enter_context(tc.tile_pool(name="keep", bufs=1))
         psum = ctx.enter_context(tc.psum_pool(name="psum", bufs=1))
+
+        def interleave(engine, grouped, raw):
+            if engine == "gpsimd":
+                nc.gpsimd.tensor_scalar(
+                    out=grouped[:, 0], in0=raw[:, 0].rearrange("p j n -> p n j"), scalar1=1.0, scalar2=0.0, op0=MULT, op1=ADD
+                )
+                return
+            dst = grouped.rearrange("p a (n i) j -> p a n j i", i=4)
+            src = raw.rearrange("p a j (n i) -> p a n j i", i=4)
+            if engine == "vector":
+                nc.vector.tensor_copy(out=dst, in_=src)
+            else:
+                nc.scalar.copy(out=dst, in_=src)
+
+        def quantise_weights(name, grouped):
+            shape = [P, grouped.shape[1], grouped.shape[2]]
+            codes = keep.tile(shape, U32, name=f"codes_{name}", align_bytes=64)
+            scales = keep.tile(shape, U8, name=f"scales_{name}", align_bytes=64)
+            nc.vector.quantize_mx(
+                out=codes[:].rearrange("p a n -> p (a n)").bitcast(FP8X4),
+                scales=scales[:].rearrange("p a n -> p (a n)"),
+                in_=grouped.rearrange("p a n j -> p (a n j)"),
+            )
+            return codes, scales
+
+        def load(raw, rows):
+            nc.sync.dma_start(out=raw, in_=rows.rearrange("(a p j) n -> p a j n", p=P, j=PACK))
+
+        blank = keep.tile([P, 1], F32, name="blank")
+        gelu_of_blank = keep.tile([P, 1], F32, name="gelu_of_blank")
+        x_scales = keep.tile([P, WINDOW], U8, name="x_scales", align_bytes=64)
+        nc.gpsimd.memset(x_scales[:], 0)
+        nc.gpsimd.memset(blank[:], 0.0)
+        nc.scalar.activation(out=gelu_of_blank[:], in_=blank[:], func=GELU)
 
         offs_sb = keep.tile([P, SLOTS // 16], U16, name="offs_sb")
         pos1_sb = keep.tile([P, T // 16], U16, name="pos1_sb")
         pos2_sb = keep.tile([P, T // 16], U16, name="pos2_sb")
         bias = keep.tile([P, BLOCKS, E], F32, name="bias")
-        warm = keep.tile([P, 1], F32, name="warm")
-        warmed = keep.tile([P, 1], F32, name="warmed")
+        x_raw = [keep.tile([P, 1, PACK, T], F32, name=f"x_raw{a}") for a in range(PASSES)]
+        for a in range(PASSES):
+            load(x_raw[a][:], xT[a * K_PASS : (a + 1) * K_PASS, :])
+            if a == 0:
+                nc.sync.dma_start(offs_sb[:], offs)
 
-        x_words = [keep.tile([P, WINDOW], U32, name=f"x_words{a}", align_bytes=64) for a in range(PASSES)]
-        x_bytes = keep.tile([P, WINDOW], U8, name="x_bytes", align_bytes=64)
-        words = keep.tile([P, PASSES, SLOTS], U32, name="words", align_bytes=64)
-        scales = keep.tile([P, SLOTS], U8, name="scales", align_bytes=64)
-        y = [keep.tile([P, SLOTS], F32, name=f"y{m}") for m in range(BLOCKS)]
-        gates = [keep.tile([P, 2, T], F32, name=f"gates{m}") for m in range(BLOCKS)]
-
-        nc.gpsimd.memset(x_bytes[:], 0)
-        nc.gpsimd.memset(warm[:], 0.0)
-        nc.scalar.activation(out=warmed[:], in_=warm[:], func=GELU)
-
-        identity = keep.tile([P, P], F32, name="identity")
-        make_identity(nc, identity[:])
-
-        def x_load(raw, a, cols):
-            rows = xT[a * K_PASS : (a + 1) * K_PASS, :].rearrange("(p j) t -> p j t", j=PACK)
-            nc.sync.dma_start(out=raw[:], in_=rows[:, :, cols])
-
-        def w_load(raw, e, k, passes):
-            rows = w[e, k * K_PASS : (k + passes) * K_PASS, :]
-            nc.sync.dma_start(out=raw[:], in_=rows.rearrange("(a p j) n -> p a j n", p=P, j=PACK))
-
-        def quantise(codes, planes, grouped):
-            nc.vector.quantize_mx(out=codes.bitcast(FP8X4), scales=planes, in_=grouped)
-
-        x_raw00 = keep.tile([P, PACK, 256], F32)
-        x_load(x_raw00, 0, slice(0, 256))
-        x_raw01 = keep.tile([P, PACK, 256], F32)
-        x_load(x_raw01, 0, slice(256, 512))
-        nc.sync.dma_start(offs_sb[:], offs)
-        x_raw10 = keep.tile([P, PACK, 512], F32)
-        x_load(x_raw10, 1, slice(0, 512))
-        x_raw20 = keep.tile([P, PACK, 512], F32)
-        x_load(x_raw20, 2, slice(0, 512))
-        x_raw30 = keep.tile([P, PACK, 512], F32)
-        x_load(x_raw30, 3, slice(0, 512))
-        w_raw00 = keep.tile([P, 2, PACK, N], F32)
-        w_load(w_raw00, 0, 0, 2)
-        w_raw01 = keep.tile([P, 2, PACK, N], F32)
-        w_load(w_raw01, 0, 2, 2)
-        w_raw10 = keep.tile([P, 2, PACK, N], F32)
-        w_load(w_raw10, 1, 0, 2)
-        w_raw11 = keep.tile([P, 2, PACK, N], F32)
-        w_load(w_raw11, 1, 2, 2)
-        w_raw20 = keep.tile([P, 2, PACK, N], F32)
-        w_load(w_raw20, 2, 0, 2)
-        w_raw21 = keep.tile([P, 2, PACK, N], F32)
-        w_load(w_raw21, 2, 2, 2)
-        nc.sync.dma_start(out=bias[:], in_=b.rearrange("(m p) e -> p m e", p=P))
-        w_raw30 = keep.tile([P, 2, PACK, N], F32)
-        w_load(w_raw30, 3, 0, 2)
-        w_raw31 = keep.tile([P, 2, PACK, N], F32)
-        w_load(w_raw31, 3, 2, 2)
+        w_raw = [[keep.tile([P, 2, PACK, N], F32, name=f"w_raw{e}{h}") for h in range(2)] for e in range(E)]
+        for e in range(E):
+            if e == LAST:
+                nc.sync.dma_start(out=bias[:], in_=b.rearrange("(m p) e -> p m e", p=P))
+            for h in range(2):
+                if (e, h) == (LAST, 1):
+                    for a in range(2):
+                        load(w_raw[e][h][:, a : a + 1], w[e, (2 + a) * K_PASS : (3 + a) * K_PASS, :])
+                else:
+                    load(w_raw[e][h][:], w[e, 2 * h * K_PASS : (2 * h + 2) * K_PASS, :])
         nc.sync.dma_start(pos1_sb[:], pos1)
         nc.sync.dma_start(pos2_sb[:], pos2)
-        nc.sync.dma_start(out=gates[0][:], in_=gate[:, 0 * P : 1 * P, :].rearrange("g p t -> p g t"))
-        nc.sync.dma_start(out=gates[1][:], in_=gate[:, 1 * P : 2 * P, :].rearrange("g p t -> p g t"))
-        def multiply(acc, e, k, codes, planes):
+        gates = [keep.tile([P, 2, T], F32, name=f"gates{m}") for m in range(BLOCKS)]
+        for m in range(BLOCKS):
+            nc.sync.dma_start(out=gates[m][:], in_=gate[:, m * P : (m + 1) * P, :].rearrange("g p t -> p g t"))
+
+        words = keep.tile([P, PASSES, SLOTS], U32, name="words", align_bytes=64)
+        scales = keep.tile([P, SLOTS], U8, name="scales", align_bytes=64)
+        for a in range(PASSES):
+            x_grouped = keep.tile([P, 1, T, PACK], BF16, name=f"x_grouped{a}", align_bytes=64)
+            x_words = keep.tile([P, WINDOW], U32, name=f"x_words{a}", align_bytes=64)
+            interleave(TOKEN_ENGINES[a], x_grouped[:], x_raw[a][:])
+            nc.vector.quantize_mx(
+                out=x_words[:, 0:T].bitcast(FP8X4),
+                scales=x_scales[4 * a :, 0:T],
+                in_=x_grouped[:].rearrange("p a t j -> p (a t j)"),
+            )
+            nc.vector.tensor_copy(words[:, a, :], x_words[:].indirect(offs_sb[:]))
+        nc.vector.tensor_copy(scales[:], x_scales[:].indirect(offs_sb[:]))
+
+        y = [keep.tile([P, SLOTS], F32, name=f"y{m}") for m in range(BLOCKS)]
+
+        def multiply(acc, e, k, codes, code_scales):
             slots = slice(e * C, (e + 1) * C)
             nc.tensor.matmul_mx(
                 out=acc,
                 lhsT=codes.bitcast(FP8X4),
-                lhsT_scale=planes,
+                lhsT_scale=code_scales,
                 rhs=words[:, k, slots].bitcast(FP8X4),
                 rhs_scale=scales[4 * k :, slots],
                 start=(k == 0),
@@ -127,103 +131,49 @@ def tile_routed_moe_kernel(tc, xT, w, b, gate, offs, pos1, pos2, out):
         def activate(e, m, acc):
             nc.scalar.activation(out=y[m][:, e * C : (e + 1) * C], in_=acc, func=GELU, bias=bias[:, m, e : e + 1])
 
-        w_grp0 = keep.tile([P, PASSES, N, PACK], BF16, align_bytes=64)
-        w_codes0 = keep.tile([P, PASSES, N], U32, align_bytes=64)
-        w_planes0 = keep.tile([P, PASSES, N], U8, align_bytes=64)
-        acc0 = psum.tile([P, BLOCKS, C], F32)
-        w_grp1 = keep.tile([P, PASSES, N, PACK], BF16, align_bytes=64)
-        w_codes1 = keep.tile([P, PASSES, N], U32, align_bytes=64)
-        w_planes1 = keep.tile([P, PASSES, N], U8, align_bytes=64)
-        acc1 = psum.tile([P, BLOCKS, C], F32)
-        w_grp2 = keep.tile([P, PASSES, N, PACK], BF16, align_bytes=64)
-        w_codes2 = keep.tile([P, PASSES, N], U32, align_bytes=64)
-        w_planes2 = keep.tile([P, PASSES, N], U8, align_bytes=64)
-        acc2 = psum.tile([P, BLOCKS, C], F32)
-        w_grp30 = keep.tile([P, 2, N, PACK], BF16, align_bytes=64)
-        w_codes30 = keep.tile([P, 2, N], U32, align_bytes=64)
-        w_planes30 = keep.tile([P, 2, N], U8, align_bytes=64)
-        w_grp32 = keep.tile([P, 1, N, PACK], BF16, align_bytes=64)
-        w_codes32 = keep.tile([P, 1, N], U32, align_bytes=64)
-        w_planes32 = keep.tile([P, 1, N], U8, align_bytes=64)
-        w_grp33 = keep.tile([P, 1, N, PACK], BF16, align_bytes=64)
-        w_codes33 = keep.tile([P, 1, N], U32, align_bytes=64)
-        w_planes33 = keep.tile([P, 1, N], U8, align_bytes=64)
+        accs = []
+        for e in range(LAST):
+            grouped = keep.tile([P, PASSES, N, PACK], BF16, name=f"w_grouped{e}", align_bytes=64)
+            for engine, k, passes in WEIGHT_ENGINES[e]:
+                a = k % 2
+                interleave(engine, grouped[:, k : k + passes], w_raw[e][k // 2][:, a : a + passes])
+            codes, code_scales = quantise_weights(f"{e}", grouped[:])
+            acc = psum.tile([P, BLOCKS, C], F32, name=f"acc{e}")
+            for m in range(BLOCKS):
+                cols = slice(m * P, (m + 1) * P)
+                for k in range(PASSES):
+                    multiply(acc[:, m], e, k, codes[:, k, cols], code_scales[:, k, cols])
+            accs.append(acc)
+        for e in range(LAST - 1):
+            for m in range(BLOCKS):
+                activate(e, m, accs[e][:, m])
+
         acc_last = [psum.tile([P, C], F32, name=f"acc_last{m}") for m in range(BLOCKS)]
-        x_grp00 = keep.tile([P, 256, PACK], BF16, align_bytes=64)
-        interleave("V", x_grp00[:], x_raw00[:])
-        quantise(x_words[0][:, 0:256], x_bytes[4 * 0 :, 0:256], x_grp00[:].rearrange("p t j -> p (t j)"))
-        x_grp01 = keep.tile([P, 256, PACK], BF16, align_bytes=64)
-        interleave("S", x_grp01[:], x_raw01[:])
-        quantise(x_words[0][:, 256:512], x_bytes[4 * 0 :, 256:512], x_grp01[:].rearrange("p t j -> p (t j)"))
-        nc.vector.tensor_copy(words[:, 0, :], x_words[0][:].indirect(offs_sb[:]))
-        x_grp10 = keep.tile([P, 512, PACK], BF16, align_bytes=64)
-        interleave("S", x_grp10[:], x_raw10[:])
-        quantise(x_words[1][:, 0:512], x_bytes[4 * 1 :, 0:512], x_grp10[:].rearrange("p t j -> p (t j)"))
-        nc.vector.tensor_copy(words[:, 1, :], x_words[1][:].indirect(offs_sb[:]))
-        x_grp20 = keep.tile([P, 512, PACK], BF16, align_bytes=64)
-        interleave("S", x_grp20[:], x_raw20[:])
-        quantise(x_words[2][:, 0:512], x_bytes[4 * 2 :, 0:512], x_grp20[:].rearrange("p t j -> p (t j)"))
-        nc.vector.tensor_copy(words[:, 2, :], x_words[2][:].indirect(offs_sb[:]))
-        x_grp30 = keep.tile([P, 512, PACK], BF16, align_bytes=64)
-        interleave("S", x_grp30[:], x_raw30[:])
-        quantise(x_words[3][:, 0:512], x_bytes[4 * 3 :, 0:512], x_grp30[:].rearrange("p t j -> p (t j)"))
-        nc.vector.tensor_copy(words[:, 3, :], x_words[3][:].indirect(offs_sb[:]))
-        nc.vector.tensor_copy(scales[:], x_bytes[:].indirect(offs_sb[:]))
-        interleave("S", w_grp0[:, 0:2], w_raw00[:])
-        interleave("S", w_grp0[:, 2:3], w_raw01[:, 0:1])
-        interleave("G", w_grp0[:, 3:4], w_raw01[:, 1:2])
-        quantise(w_codes0[:].rearrange("p a n -> p (a n)"), w_planes0[:].rearrange("p a n -> p (a n)"), w_grp0[:].rearrange("p a n j -> p (a n j)"))
+        for engine, k, passes in (("scalar", 0, 2), ("vector", 2, 1)):
+            grouped = keep.tile([P, passes, N, PACK], BF16, name=f"w_grouped{LAST}{k}", align_bytes=64)
+            interleave(engine, grouped[:], w_raw[LAST][k // 2][:, 0:passes])
+            codes, code_scales = quantise_weights(f"{LAST}{k}", grouped[:])
+            for m in range(BLOCKS):
+                cols = slice(m * P, (m + 1) * P)
+                for a in range(passes):
+                    multiply(acc_last[m][:], LAST, k + a, codes[:, a, cols], code_scales[:, a, cols])
+        k = PASSES - 1
+        for m, engine in enumerate(("vector", "scalar")):
+            grouped = keep.tile([P, 1, P, PACK], BF16, name=f"w_grouped{LAST}{k}{m}", align_bytes=64)
+            interleave(engine, grouped[:], w_raw[LAST][1][:, 1:2, :, m * P : (m + 1) * P])
+            codes, code_scales = quantise_weights(f"{LAST}{k}{m}", grouped[:])
+            multiply(acc_last[m][:], LAST, k, codes[:, 0], code_scales[:, 0])
+
         for m in range(BLOCKS):
-            for k in range(PASSES):
-                multiply(acc0[:, m], 0, k, w_codes0[:, k, m * P : (m + 1) * P], w_planes0[:, k, m * P : (m + 1) * P])
-        interleave("S", w_grp1[:, 0:2], w_raw10[:])
-        interleave("S", w_grp1[:, 2:3], w_raw11[:, 0:1])
-        interleave("G", w_grp1[:, 3:4], w_raw11[:, 1:2])
-        quantise(w_codes1[:].rearrange("p a n -> p (a n)"), w_planes1[:].rearrange("p a n -> p (a n)"), w_grp1[:].rearrange("p a n j -> p (a n j)"))
+            activate(LAST - 1, m, accs[LAST - 1][:, m])
         for m in range(BLOCKS):
-            for k in range(PASSES):
-                multiply(acc1[:, m], 1, k, w_codes1[:, k, m * P : (m + 1) * P], w_planes1[:, k, m * P : (m + 1) * P])
-        interleave("S", w_grp2[:, 0:2], w_raw20[:])
-        interleave("V", w_grp2[:, 2:4], w_raw21[:])
-        quantise(w_codes2[:].rearrange("p a n -> p (a n)"), w_planes2[:].rearrange("p a n -> p (a n)"), w_grp2[:].rearrange("p a n j -> p (a n j)"))
+            activate(LAST, m, acc_last[m][:])
+
         for m in range(BLOCKS):
-            for k in range(PASSES):
-                multiply(acc2[:, m], 2, k, w_codes2[:, k, m * P : (m + 1) * P], w_planes2[:, k, m * P : (m + 1) * P])
-        for m in range(BLOCKS):
-            activate(0, m, acc0[:, m])
-        for m in range(BLOCKS):
-            activate(1, m, acc1[:, m])
-        interleave("S", w_grp30[:], w_raw30[:])
-        quantise(w_codes30[:].rearrange("p a n -> p (a n)"), w_planes30[:].rearrange("p a n -> p (a n)"), w_grp30[:].rearrange("p a n j -> p (a n j)"))
-        for m in range(BLOCKS):
-            for k in range(2):
-                multiply(acc_last[m][:], 3, k, w_codes30[:, k, m * P : (m + 1) * P], w_planes30[:, k, m * P : (m + 1) * P])
-        interleave("V", w_grp32[:], w_raw31[:, 0:1])
-        interleave("S", w_grp33[:], w_raw31[:, 1:2])
-        quantise(w_codes32[:].rearrange("p a n -> p (a n)"), w_planes32[:].rearrange("p a n -> p (a n)"), w_grp32[:].rearrange("p a n j -> p (a n j)"))
-        for m in range(BLOCKS):
-            multiply(acc_last[m][:], 3, 2, w_codes32[:, 0, m * P : (m + 1) * P], w_planes32[:, 0, m * P : (m + 1) * P])
-        quantise(w_codes33[:].rearrange("p a n -> p (a n)"), w_planes33[:].rearrange("p a n -> p (a n)"), w_grp33[:].rearrange("p a n j -> p (a n j)"))
-        for m in range(BLOCKS):
-            multiply(acc_last[m][:], 3, 3, w_codes33[:, 0, m * P : (m + 1) * P], w_planes33[:, 0, m * P : (m + 1) * P])
-        for m in range(BLOCKS):
-            activate(2, m, acc2[:, m])
-        activate(3, 0, acc_last[0][:])
-        activate(3, 1, acc_last[1][:])
-        first0 = keep.tile([P, T], F32)
-        second0 = keep.tile([P, T], F32)
-        total0 = keep.tile([P, T], F32)
-        nc.vector.tensor_tensor(first0[:], y[0][:].indirect(pos1_sb[:]), gates[0][:, 0], MULT)
-        nc.vector.tensor_tensor(second0[:], y[0][:].indirect(pos2_sb[:]), gates[0][:, 1], MULT)
-        both0 = psum.tile([P, T], F32)
-        nc.tensor.matmul(both0[:], identity[:], first0[:], start=True, stop=False)
-        nc.tensor.matmul(both0[:], identity[:], second0[:], start=False, stop=True)
-        nc.scalar.copy(out=total0[:], in_=both0[:])
-        nc.sync.dma_start(out=out[0 * P : 1 * P, :], in_=total0[:])
-        first1 = keep.tile([P, T], F32)
-        second1 = keep.tile([P, T], F32)
-        total1 = keep.tile([P, T], F32)
-        nc.vector.tensor_tensor(first1[:], y[1][:].indirect(pos1_sb[:]), gates[1][:, 0], MULT)
-        nc.vector.tensor_tensor(second1[:], y[1][:].indirect(pos2_sb[:]), gates[1][:, 1], MULT)
-        nc.vector.tensor_tensor(total1[:], first1[:], second1[:], ADD)
-        nc.sync.dma_start(out=out[1 * P : 2 * P, :], in_=total1[:])
+            first = keep.tile([P, T], F32, name=f"first{m}")
+            second = keep.tile([P, T], F32, name=f"second{m}")
+            total = keep.tile([P, T], F32, name=f"total{m}")
+            nc.vector.tensor_tensor(first[:], y[m][:].indirect(pos1_sb[:]), gates[m][:, 0], MULT)
+            nc.vector.tensor_tensor(second[:], y[m][:].indirect(pos2_sb[:]), gates[m][:, 1], MULT)
+            nc.vector.tensor_tensor(total[:], first[:], second[:], ADD)
+            nc.sync.dma_start(out=out[m * P : (m + 1) * P, :], in_=total[:])

from contextlib import ExitStack

import concourse.mybir as mybir

K, T, E, C, N = 2048, 512, 4, 256, 256
FLOPS = 2 * E * C * K * N

F32 = mybir.dt.float32
BF16 = mybir.dt.bfloat16
U32 = mybir.dt.uint32
U16 = mybir.dt.uint16
U8 = mybir.dt.uint8
FP8X4 = mybir.dt.float8_e4m3fn_x4
MULT = mybir.AluOpType.mult
ADD = mybir.AluOpType.add
GELU = mybir.ActivationFunctionType.Gelu_apprx_tanh

P = 128
PACK = 4
K_PASS = P * PACK
PASSES = K // K_PASS
BLOCKS = N // P
SLOTS = E * C
LAST = E - 1

WINDOW = 1376

TOKEN_ENGINES = ("vector", "scalar", "scalar", "scalar")
WEIGHT_ENGINES = (
    (("scalar", 0, 2), ("scalar", 2, 1), ("gpsimd", 3, 1)),
    (("scalar", 0, 2), ("scalar", 2, 1), ("gpsimd", 3, 1)),
    (("scalar", 0, 2), ("vector", 2, 2)),
)


def tile_routed_moe_kernel(tc, xT, w, b, gate, offs, pos1, pos2, out):
    nc = tc.nc

    with ExitStack() as ctx:
        keep = ctx.enter_context(tc.tile_pool(name="keep", bufs=1))
        psum = ctx.enter_context(tc.psum_pool(name="psum", bufs=1))

        def interleave(engine, grouped, raw):
            if engine == "gpsimd":
                nc.gpsimd.tensor_scalar(
                    out=grouped[:, 0], in0=raw[:, 0].rearrange("p j n -> p n j"), scalar1=1.0, scalar2=0.0, op0=MULT, op1=ADD
                )
                return
            dst = grouped.rearrange("p a (n i) j -> p a n j i", i=4)
            src = raw.rearrange("p a j (n i) -> p a n j i", i=4)
            if engine == "vector":
                nc.vector.tensor_copy(out=dst, in_=src)
            else:
                nc.scalar.copy(out=dst, in_=src)

        def quantise_weights(name, grouped):
            shape = [P, grouped.shape[1], grouped.shape[2]]
            codes = keep.tile(shape, U32, name=f"codes_{name}", align_bytes=64)
            scales = keep.tile(shape, U8, name=f"scales_{name}", align_bytes=64)
            nc.vector.quantize_mx(
                out=codes[:].rearrange("p a n -> p (a n)").bitcast(FP8X4),
                scales=scales[:].rearrange("p a n -> p (a n)"),
                in_=grouped.rearrange("p a n j -> p (a n j)"),
            )
            return codes, scales

        def load(raw, rows):
            nc.sync.dma_start(out=raw, in_=rows.rearrange("(a p j) n -> p a j n", p=P, j=PACK))

        blank = keep.tile([P, 1], F32, name="blank")
        gelu_of_blank = keep.tile([P, 1], F32, name="gelu_of_blank")
        x_scales = keep.tile([P, WINDOW], U8, name="x_scales", align_bytes=64)
        nc.gpsimd.memset(x_scales[:], 0)
        nc.gpsimd.memset(blank[:], 0.0)
        nc.scalar.activation(out=gelu_of_blank[:], in_=blank[:], func=GELU)

        offs_sb = keep.tile([P, SLOTS // 16], U16, name="offs_sb")
        pos1_sb = keep.tile([P, T // 16], U16, name="pos1_sb")
        pos2_sb = keep.tile([P, T // 16], U16, name="pos2_sb")
        bias = keep.tile([P, BLOCKS, E], F32, name="bias")
        x_raw = [keep.tile([P, 1, PACK, T], F32, name=f"x_raw{a}") for a in range(PASSES)]
        for a in range(PASSES):
            load(x_raw[a][:], xT[a * K_PASS : (a + 1) * K_PASS, :])
            if a == 0:
                nc.sync.dma_start(offs_sb[:], offs)

        w_raw = [[keep.tile([P, 2, PACK, N], F32, name=f"w_raw{e}{h}") for h in range(2)] for e in range(E)]
        for e in range(E):
            if e == LAST:
                nc.sync.dma_start(out=bias[:], in_=b.rearrange("(m p) e -> p m e", p=P))
            for h in range(2):
                if (e, h) == (LAST, 1):
                    for a in range(2):
                        load(w_raw[e][h][:, a : a + 1], w[e, (2 + a) * K_PASS : (3 + a) * K_PASS, :])
                else:
                    load(w_raw[e][h][:], w[e, 2 * h * K_PASS : (2 * h + 2) * K_PASS, :])
        nc.sync.dma_start(pos1_sb[:], pos1)
        nc.sync.dma_start(pos2_sb[:], pos2)
        gates = [keep.tile([P, 2, T], F32, name=f"gates{m}") for m in range(BLOCKS)]
        for m in range(BLOCKS):
            nc.sync.dma_start(out=gates[m][:], in_=gate[:, m * P : (m + 1) * P, :].rearrange("g p t -> p g t"))

        words = keep.tile([P, PASSES, SLOTS], U32, name="words", align_bytes=64)
        scales = keep.tile([P, SLOTS], U8, name="scales", align_bytes=64)
        for a in range(PASSES):
            x_grouped = keep.tile([P, 1, T, PACK], BF16, name=f"x_grouped{a}", align_bytes=64)
            x_words = keep.tile([P, WINDOW], U32, name=f"x_words{a}", align_bytes=64)
            interleave(TOKEN_ENGINES[a], x_grouped[:], x_raw[a][:])
            nc.vector.quantize_mx(
                out=x_words[:, 0:T].bitcast(FP8X4),
                scales=x_scales[4 * a :, 0:T],
                in_=x_grouped[:].rearrange("p a t j -> p (a t j)"),
            )
            nc.vector.tensor_copy(words[:, a, :], x_words[:].indirect(offs_sb[:]))
        nc.vector.tensor_copy(scales[:], x_scales[:].indirect(offs_sb[:]))

        y = [keep.tile([P, SLOTS], F32, name=f"y{m}") for m in range(BLOCKS)]

        def multiply(acc, e, k, codes, code_scales):
            slots = slice(e * C, (e + 1) * C)
            nc.tensor.matmul_mx(
                out=acc,
                lhsT=codes.bitcast(FP8X4),
                lhsT_scale=code_scales,
                rhs=words[:, k, slots].bitcast(FP8X4),
                rhs_scale=scales[4 * k :, slots],
                start=(k == 0),
                stop=(k == PASSES - 1),
            )

        def activate(e, m, acc):
            nc.scalar.activation(out=y[m][:, e * C : (e + 1) * C], in_=acc, func=GELU, bias=bias[:, m, e : e + 1])

        accs = []
        for e in range(LAST):
            grouped = keep.tile([P, PASSES, N, PACK], BF16, name=f"w_grouped{e}", align_bytes=64)
            for engine, k, passes in WEIGHT_ENGINES[e]:
                a = k % 2
                interleave(engine, grouped[:, k : k + passes], w_raw[e][k // 2][:, a : a + passes])
            codes, code_scales = quantise_weights(f"{e}", grouped[:])
            acc = psum.tile([P, BLOCKS, C], F32, name=f"acc{e}")
            for m in range(BLOCKS):
                cols = slice(m * P, (m + 1) * P)
                for k in range(PASSES):
                    multiply(acc[:, m], e, k, codes[:, k, cols], code_scales[:, k, cols])
            accs.append(acc)
        for e in range(LAST - 1):
            for m in range(BLOCKS):
                activate(e, m, accs[e][:, m])

        acc_last = [psum.tile([P, C], F32, name=f"acc_last{m}") for m in range(BLOCKS)]
        for engine, k, passes in (("scalar", 0, 2), ("vector", 2, 1)):
            grouped = keep.tile([P, passes, N, PACK], BF16, name=f"w_grouped{LAST}{k}", align_bytes=64)
            interleave(engine, grouped[:], w_raw[LAST][k // 2][:, 0:passes])
            codes, code_scales = quantise_weights(f"{LAST}{k}", grouped[:])
            for m in range(BLOCKS):
                cols = slice(m * P, (m + 1) * P)
                for a in range(passes):
                    multiply(acc_last[m][:], LAST, k + a, codes[:, a, cols], code_scales[:, a, cols])
        k = PASSES - 1
        for m, engine in enumerate(("vector", "scalar")):
            grouped = keep.tile([P, 1, P, PACK], BF16, name=f"w_grouped{LAST}{k}{m}", align_bytes=64)
            interleave(engine, grouped[:], w_raw[LAST][1][:, 1:2, :, m * P : (m + 1) * P])
            codes, code_scales = quantise_weights(f"{LAST}{k}{m}", grouped[:])
            multiply(acc_last[m][:], LAST, k, codes[:, 0], code_scales[:, 0])

        for m in range(BLOCKS):
            activate(LAST - 1, m, accs[LAST - 1][:, m])
        for m in range(BLOCKS):
            activate(LAST, m, acc_last[m][:])

        for m in range(BLOCKS):
            first = keep.tile([P, T], F32, name=f"first{m}")
            second = keep.tile([P, T], F32, name=f"second{m}")
            total = keep.tile([P, T], F32, name=f"total{m}")
            nc.vector.tensor_tensor(first[:], y[m][:].indirect(pos1_sb[:]), gates[m][:, 0], MULT)
            nc.vector.tensor_tensor(second[:], y[m][:].indirect(pos2_sb[:]), gates[m][:, 1], MULT)
            nc.vector.tensor_tensor(total[:], first[:], second[:], ADD)
            nc.sync.dma_start(out=out[m * P : (m + 1) * P, :], in_=total[:])
